import numpy as np
import ml_dtypes


def mxq(x, axis, fmt="e4m3"):
    dtype, down = {"e4m3": (ml_dtypes.float8_e4m3fn, 7), "e5m2": (ml_dtypes.float8_e5m2, 14)}[fmt]
    v = np.moveaxis(np.asarray(x, np.float32).astype(ml_dtypes.bfloat16).astype(np.float64), axis, -1)
    blocks = v.reshape(v.shape[:-1] + (-1, 32))
    amax = np.abs(blocks).max(-1, keepdims=True)
    byte = np.maximum(np.where(amax > 0, np.frexp(amax)[1] - 1 + 127, 0) - down, 1)
    scale = np.exp2(byte - 127.0)
    codes = (blocks / scale).astype(np.float32).astype(dtype).astype(np.float64)
    return np.moveaxis((codes * scale).reshape(v.shape), -1, axis)


WIDE = False


def mx_kscale(k):
    if not WIDE:
        return np.ones(k)
    levels = np.array([10, -10, 5, -5, 0])
    if k % 512:
        return np.exp2(np.random.permutation(np.resize(levels, k // 32))).repeat(32)
    a = np.empty((k // 512, 16))
    for p in range(k // 512):
        a[p, :8] = np.random.permutation(np.resize(levels, 8))
        for g in range(8):
            far = levels[np.abs(levels - a[p, g]) >= 10]
            a[p, g + 8] = far[np.random.randint(len(far))]
    return np.exp2(a.ravel()).repeat(32)


def f64(x):
    return np.asarray(x).astype(np.float64)


def striped(idx):
    return np.tile(idx.reshape(-1, 16).T, (8, 1)).astype(np.uint16)


def unstriped(offs):
    return offs[:16].T.reshape(-1).astype(np.int64)


def striped8(idx):
    return np.concatenate([x.reshape(-1, 16).T for x in idx]).astype(np.uint16)


def runs(offs, k):
    lists = np.stack([offs[16 * r : 16 * r + 16].T.reshape(-1) for r in range(8)]).astype(np.int64)
    return lists[np.arange(k) % 512 // 64]


def pack_weight(w):
    k, n = w.shape
    w = f64(np.asarray(w, np.float32).astype(ml_dtypes.bfloat16)).reshape(k // 32, 32, n)
    amax = np.abs(w).max(1)
    byte = np.clip(np.where(amax > 0, np.frexp(amax)[1] - 1 + 127 - 7, 1), 1, 254)
    scaled = (w * np.exp2(127.0 - byte)[:, None, :]).reshape(k, n).astype(np.float32)
    words = np.ascontiguousarray(scaled.reshape(k // 512, 128, 4, n).transpose(0, 1, 3, 2)).astype(ml_dtypes.float8_e4m3fn).view(np.uint8)
    return words, np.ascontiguousarray(byte.astype(np.uint8).reshape(k // 512, 16, n))


def unpack_weight(words, scales):
    g, p, n, _ = words.shape
    vals = np.ascontiguousarray(words).view(ml_dtypes.float8_e4m3fn).astype(np.float64) * np.repeat(np.exp2(scales.astype(np.float64) - 127.0), 8, axis=1)[..., None]
    return vals.transpose(0, 1, 3, 2).reshape(g * 512, n)


K, T, S, N, G, H, W = 512, 1024, 512, 512, 2048, 512, 256


def setup_inputs():
    n = np.random.standard_normal
    s = mx_kscale(K)[:, None]
    u = mx_kscale(S)
    packed_xT = pack_weight(n((K, T)) * s)
    packed_dT = pack_weight(n((K, G)) / s)
    perm = np.random.permutation(S)
    perm2 = np.random.permutation(S)
    return {
        "x_words": packed_xT[0],
        "x_scales": packed_xT[1],
        "d_words": packed_dT[0],
        "d_scales": packed_dT[1],
        "gn": (np.random.uniform(0.5, 1.5, (H, 1)) * u[:, None]).astype(np.float32),
        "w1": (n((H, N)) / np.sqrt(H) / u[:, None]).astype(np.float32),
        "offs": striped(np.random.permutation(T)[:S]),
        "k1": striped8(np.random.randint(0, G, (8, H))),
        "hz": striped8(np.random.randint(0, T, (8, S))),
        "k2": striped8(np.random.randint(0, G, (8, H))),
        "n1": striped(perm[:W]),
        "n2": striped(perm[W:]),
        "n3": striped(perm2[:W]),
        "n4": striped(perm2[W:]),
        "n5": striped(np.random.permutation(S)),
        "n6": striped(np.random.permutation(S)),
        "n7": striped(np.random.permutation(S)),
    }


def reference(x_words, x_scales, d_words, d_scales, gn, w1, offs, k1, hz, k2, n1, n2, n3, n4, n5, n6, n7):
    d_k1 = unpack_weight(d_words, d_scales)[np.arange(K)[:, None], runs(k1, K)]
    xq = unpack_weight(x_words, x_scales)[:, unstriped(offs)]
    d_k2 = unpack_weight(d_words, d_scales)[np.arange(K)[:, None], runs(k2, K)]
    x_hz = unpack_weight(x_words, x_scales)[np.arange(K)[:, None], runs(hz, K)]
    h = 0.0625 * (d_k1.T @ xq + d_k2.T @ x_hz)
    pa = h[:, unstriped(n1)]
    pb = h[:, unstriped(n2)]
    rb = np.maximum(pa, pb)
    ua = np.zeros((H, S))
    ua[:, unstriped(n3)] = pb
    ub = ua.copy()
    ub[:, unstriped(n4)] = rb
    z = f64(gn) * (ub - h[:, unstriped(n5)])
    h2 = mxq(f64(w1), 0, "e4m3").T @ mxq(z, 0, "e4m3")
    ds = np.zeros((N, S))
    ds[:, unstriped(n6)] = h2
    ds2 = np.zeros((N, S))
    ds2[:, unstriped(n7)] = h2
    return np.maximum(ds, ds2)

@@ -1,0 +1,212 @@
+from contextlib import ExitStack
+
+import concourse.mybir as mybir
+
+K, T, S, N, G, H, W = 512, 1024, 512, 512, 2048, 512, 256
+FLOPS = 2 * K * H * S * 2 + 2 * H * N * S
+
+F32 = mybir.dt.float32
+BF16 = mybir.dt.bfloat16
+I32 = mybir.dt.int32
+U32 = mybir.dt.uint32
+U16 = mybir.dt.uint16
+U8 = mybir.dt.uint8
+FP8X4 = mybir.dt.float8_e4m3fn_x4
+ALU = mybir.AluOpType
+COPY = mybir.ActivationFunctionType.Copy
+
+P = 128
+PACK = 4
+FIRST = 128
+REST = S - FIRST
+
+
+def tile_picked_mthzncpswsendtwo_none_p_kernel(
+    tc, x_words, x_scales, d_words, d_scales, gn, w1, offs, k1, hz, k2, n1, n2, n3, n4, n5, n6, n7, out
+):
+    nc = tc.nc
+    with ExitStack() as ctx:
+        lists = ctx.enter_context(tc.tile_pool(name="lists", bufs=1))
+        keep = ctx.enter_context(tc.tile_pool(name="keep", bufs=1))
+        psum = ctx.enter_context(tc.psum_pool(name="psum", bufs=1))
+
+        def load_list(name, src):
+            t = lists.tile(list(src.shape), U16, name=name)
+            nc.sync.dma_start(t[:], src)
+            return t
+
+        d_bytes = keep.tile([P, G], U8, name="d_bytes", align_bytes=64)
+        x_bytes = keep.tile([P, T], U8, name="x_bytes", align_bytes=64)
+        planes = keep.tile([P, 4, S], U8, name="planes", align_bytes=64)
+        nc.vector.memset(d_bytes[:].bitcast(I32), 0)
+        nc.vector.memset(x_bytes[:].bitcast(I32), 0)
+        nc.vector.memset(planes[:].rearrange("p l s -> p (l s)").bitcast(I32), 0)
+        nc.scalar.dma_start(d_bytes[0:P:8, :].bitcast(I32), d_scales[0].bitcast(I32))
+        nc.scalar.dma_start(x_bytes[0:P:8, :].bitcast(I32), x_scales[0].bitcast(I32))
+
+        k1_l = load_list("k1_l", k1)
+        k2_l = load_list("k2_l", k2)
+        hz_l = load_list("hz_l", hz)
+        offs_l = load_list("offs_l", offs)
+
+        x_tab = keep.tile([P, T], U32, name="x_tab", align_bytes=64)
+        d_tab = keep.tile([P, G], U32, name="d_tab", tag="big", align_bytes=64)
+        nc.sync.dma_start(x_tab[:].bitcast(I32), x_words[0].rearrange("p c r -> p (c r)").bitcast(I32))
+        nc.sync.dma_start(d_tab[:].bitcast(I32), d_words[0].rearrange("p c r -> p (c r)").bitcast(I32))
+
+        n1_l = load_list("n1_l", n1)
+        n2_l = load_list("n2_l", n2)
+        n5_l = load_list("n5_l", n5)
+        n3_l = load_list("n3_l", n3)
+        n4_l = load_list("n4_l", n4)
+        gain = keep.tile([P, PACK], F32, name="gain")
+        nc.sync.dma_start(gain[:], gn.rearrange("(p t) o -> p (t o)", t=PACK))
+        n6_l = load_list("n6_l", n6)
+        n7_l = load_list("n7_l", n7)
+
+        got_bytes = keep.tile([P, 4, S], U8, name="got_bytes", align_bytes=64)
+        nc.vector.tensor_copy(got_bytes[:, 0, :], d_bytes[:].indirect(k1_l[:]))
+        nc.vector.tensor_copy(got_bytes[:, 1, :], d_bytes[:].indirect(k2_l[:]))
+        nc.vector.tensor_copy(got_bytes[:, 2, :], x_bytes[:].indirect(offs_l[:]))
+        nc.vector.tensor_copy(got_bytes[:, 3, :], x_bytes[:].indirect(hz_l[:]))
+        got_flat = got_bytes[:].rearrange("p l s -> p (l s)").bitcast(I32)
+        planes_flat = planes[:].rearrange("p l s -> p (l s)").bitcast(I32)
+        for r in range(4):
+            nc.scalar.dma_start(planes_flat[r:P:32, :], got_flat[8 * r : P : 32, :])
+
+        x_got = keep.tile([P, 2, S], U32, name="x_got", align_bytes=64)
+        d_got = keep.tile([P, 2, H], U32, name="d_got", align_bytes=64)
+        nc.vector.tensor_copy(x_got[:, 0, :], x_tab[:].indirect(offs_l[:]))
+        nc.vector.tensor_copy(d_got[:, 0, :], d_tab[:].indirect(k1_l[:]))
+        nc.vector.tensor_copy(d_got[:, 1, :], d_tab[:].indirect(k2_l[:]))
+
+        d_dealt = [keep.tile([P, 2, P], U32, name=f"d_dealt{t}", align_bytes=64) for t in range(PACK)]
+        b_dealt = [keep.tile([P, 2, P], U8, name=f"b_dealt{t}", align_bytes=64) for t in range(PACK)]
+        h_ps = [psum.tile([P, S], F32, name=f"h_ps{t}") for t in range(PACK)]
+
+        def deal_words(t):
+            nc.vector.tensor_copy(d_dealt[t][:], d_got[:].rearrange("p l (m t) -> p l t m", t=PACK)[:, :, t, :])
+
+        def deal_bytes(t):
+            nc.vector.tensor_copy(b_dealt[t][:], planes[:, 0:2, :].rearrange("p l (m t) -> p l t m", t=PACK)[:, :, t, :])
+
+        def first_product(t):
+            for l in range(2):
+                nc.tensor.matmul_mx(
+                    out=h_ps[t][:],
+                    lhsT=d_dealt[t][:, l, :].bitcast(FP8X4),
+                    lhsT_scale=b_dealt[t][:, l, :],
+                    rhs=x_got[:, l, :].bitcast(FP8X4),
+                    rhs_scale=planes[:, 2 + l, :],
+                    start=(l == 0),
+                    stop=(l == 1),
+                )
+
+        deal_words(0)
+        deal_bytes(0)
+        nc.vector.tensor_copy(x_got[:, 1, :], x_tab[:].indirect(hz_l[:]))
+        first_product(0)
+
+        w_raw = keep.tile([P, PACK, N], F32, name="w_raw", tag="big", align_bytes=64)
+
+        h = [keep.tile([P, S], F32, name=f"h{t}") for t in range(PACK)]
+        pa = [keep.tile([P, W], F32, name=f"pa{t}", tag=f"pa{t}") for t in range(PACK)]
+        pb = [keep.tile([P, W], F32, name=f"pb{t}", tag=f"pb{t}") for t in range(PACK)]
+        rb = [keep.tile([P, W], F32, name=f"rb{t}") for t in range(PACK)]
+        ub = [keep.tile([P, S], F32, name=f"ub{t}") for t in range(PACK)]
+        h5a = keep.tile([P, PACK, FIRST], F32, name="h5a")
+
+        def larger(t):
+            nc.vector.tensor_tensor(rb[t][:], pa[t][:], pb[t][:], ALU.max)
+            nc.scalar.activation(ub[t][:].indirect(n4_l[:]), rb[t][:], COPY)
+
+        for t in range(PACK):
+            nc.vector.tensor_scalar_mul(h[t][:], h_ps[t][:], 0.0625)
+            nc.scalar.activation(pa[t][:], h[t][:].indirect(n1_l[:]), COPY)
+            nc.vector.tensor_copy(pb[t][:], h[t][:].indirect(n2_l[:]))
+            nc.scalar.activation(h5a[:, t, :], h[t][:].indirect(n5_l[:, 0 : FIRST // 16]), COPY)
+            nc.scalar.activation(ub[t][:].indirect(n3_l[:]), pb[t][:], COPY)
+            if t + 1 < PACK:
+                deal_words(t + 1)
+                deal_bytes(t + 1)
+                first_product(t + 1)
+            if t == 0:
+                nc.sync.dma_start(w_raw[:], w1.rearrange("(p t) m -> p t m", t=PACK))
+            if t > 0:
+                larger(t - 1)
+        larger(PACK - 1)
+
+        w_bf = keep.tile([P, N, PACK], BF16, name="w_bf", align_bytes=64)
+        w_codes = keep.tile([P, N], U32, name="w_codes", align_bytes=64)
+        w_scale = keep.tile([P, N], U8, name="w_scale", align_bytes=64)
+        for half in range(2):
+            cols = slice(half * 256, (half + 1) * 256)
+            nc.vector.tensor_copy(
+                w_bf[:, cols, :].rearrange("p (c i) t -> p c t i", i=4),
+                w_raw[:, :, cols].rearrange("p t (c i) -> p c t i", i=4),
+            )
+        for half in range(2):
+            cols = slice(half * 256, (half + 1) * 256)
+            nc.vector.quantize_mx(
+                out=w_codes[:, cols].bitcast(FP8X4), scales=w_scale[:, cols],
+                in_=w_bf[:, cols, :].rearrange("p c t -> p (c t)"),
+            )
+
+        h5b = keep.tile([P, PACK, REST], F32, name="h5b", tag=f"pb{PACK - 1}")
+        for t in range(PACK):
+            nc.scalar.activation(h5b[:, t, :], h[t][:].indirect(n5_l[:, FIRST // 16 : S // 16]), COPY)
+
+        z_codes = keep.tile([P, S], U32, name="z_codes", align_bytes=64)
+        z_scale = keep.tile([P, S], U8, name="z_scale", align_bytes=64)
+        h2_ps = [psum.tile([P, S], F32, name=f"h2_ps{m}") for m in range(PACK)]
+        ds = [keep.tile([P, S], F32, name=f"ds{m}") for m in range(PACK)]
+        ds2 = [keep.tile([P, S], F32, name=f"dt{m}") for m in range(PACK)]
+
+        def second_product(m, c0, c1):
+            nc.tensor.matmul_mx(
+                out=h2_ps[m][:, c0:c1],
+                lhsT=w_codes[:, m * P : (m + 1) * P].bitcast(FP8X4),
+                lhsT_scale=w_scale[:, m * P : (m + 1) * P],
+                rhs=z_codes[:, c0:c1].bitcast(FP8X4),
+                rhs_scale=z_scale[:, c0:c1],
+                start=True,
+                stop=True,
+            )
+
+        da = keep.tile([P, PACK, FIRST], F32, name="da", tag=f"pa{PACK - 1}")
+        za = keep.tile([P, FIRST, PACK], BF16, name="za", align_bytes=64)
+        for t in range(PACK):
+            nc.vector.tensor_tensor(da[:, t, :], ub[t][:, 0:FIRST], h5a[:, t, :], ALU.subtract)
+            nc.vector.tensor_scalar_mul(za[:, :, t], da[:, t, :], gain[:, t : t + 1])
+        nc.vector.quantize_mx(out=z_codes[:, 0:FIRST].bitcast(FP8X4), scales=z_scale[:, 0:FIRST],
+                              in_=za[:].rearrange("p c t -> p (c t)"))
+        h2a = [keep.tile([P, FIRST], F32, name=f"h2a{m}") for m in range(PACK)]
+        for m in range(PACK):
+            second_product(m, 0, FIRST)
+            nc.vector.tensor_copy(h2a[m][:], h2_ps[m][:, 0:FIRST])
+            nc.scalar.activation(ds[m][:].indirect(n6_l[:, 0 : FIRST // 16]), h2a[m][:], COPY)
+            nc.scalar.activation(ds2[m][:].indirect(n7_l[:, 0 : FIRST // 16]), h2a[m][:], COPY)
+
+        db = keep.tile([P, PACK, REST], F32, name="db")
+        zb = keep.tile([P, REST, PACK], BF16, name="zb", align_bytes=64)
+        for t in range(PACK):
+            nc.vector.tensor_tensor(db[:, t, :], ub[t][:, FIRST:S], h5b[:, t, :], ALU.subtract)
+        nc.vector.tensor_tensor(
+            zb[:].rearrange("p (c i) t -> p c t i", i=4),
+            db[:].rearrange("p t (c i) -> p c t i", i=4),
+            gain[:].unsqueeze(1).unsqueeze(3).broadcast_to([P, REST // 4, PACK, 4]),
+            ALU.mult,
+        )
+        nc.vector.quantize_mx(out=z_codes[:, FIRST:S].bitcast(FP8X4), scales=z_scale[:, FIRST:S],
+                              in_=zb[:].rearrange("p c t -> p (c t)"))
+        h2b = [keep.tile([P, REST], F32, name=f"h2b{m}") for m in range(PACK)]
+        res = [keep.tile([P, S], F32, name=f"res{m}") for m in range(PACK)]
+        for m in range(PACK):
+            second_product(m, FIRST, FIRST + 256)
+            second_product(m, FIRST + 256, S)
+            nc.vector.tensor_copy(h2b[m][:], h2_ps[m][:, FIRST:S])
+        for m in range(PACK):
+            nc.scalar.activation(ds[m][:].indirect(n6_l[:, FIRST // 16 : S // 16]), h2b[m][:], COPY)
+            nc.scalar.activation(ds2[m][:].indirect(n7_l[:, FIRST // 16 : S // 16]), h2b[m][:], COPY)
+            nc.vector.tensor_tensor(res[m][:], ds[m][:], ds2[m][:], ALU.max)
+            nc.sync.dma_start(out[m * P : (m + 1) * P, :], res[m][:])

@@ -35,68 +35,68 @@ def tile_picked_mthzncpswsendtwo_none_p_kernel(
             nc.sync.dma_start(t[:], src)
             return t
 
-        d_bytes = keep.tile([P, G], U8, name="d_bytes", align_bytes=64)
-        x_bytes = keep.tile([P, T], U8, name="x_bytes", align_bytes=64)
+        d_bytes = keep.tile([P, G], U8, name="d_bytes", tag="d_bytes", align_bytes=64)
+        x_bytes = keep.tile([P, T], U8, name="x_bytes", tag="x_bytes", align_bytes=64)
         planes = keep.tile([P, 4, S], U8, name="planes", align_bytes=64)
+        nc.gpsimd.memset(x_bytes[:].bitcast(I32), 0)
         nc.vector.memset(d_bytes[:].bitcast(I32), 0)
-        nc.vector.memset(x_bytes[:].bitcast(I32), 0)
-        nc.vector.memset(planes[:].rearrange("p l s -> p (l s)").bitcast(I32), 0)
-        nc.scalar.dma_start(d_bytes[0:P:8, :].bitcast(I32), d_scales[0].bitcast(I32))
         nc.scalar.dma_start(x_bytes[0:P:8, :].bitcast(I32), x_scales[0].bitcast(I32))
-
+        nc.scalar.dma_start(d_bytes[0:P:8, :].bitcast(I32), d_scales[0].bitcast(I32))
+        offs_l = load_list("offs_l", offs)
+        hz_l = load_list("hz_l", hz)
         k1_l = load_list("k1_l", k1)
         k2_l = load_list("k2_l", k2)
-        hz_l = load_list("hz_l", hz)
-        offs_l = load_list("offs_l", offs)
+        nc.vector.memset(planes[:].rearrange("p l s -> p (l s)").bitcast(I32), 0)
 
-        x_tab = keep.tile([P, T], U32, name="x_tab", align_bytes=64)
+        x_tab = keep.tile([P, T], U32, name="x_tab", tag="x_tab", align_bytes=64)
         d_tab = keep.tile([P, G], U32, name="d_tab", tag="big", align_bytes=64)
-        nc.sync.dma_start(x_tab[:].bitcast(I32), x_words[0].rearrange("p c r -> p (c r)").bitcast(I32))
-        nc.sync.dma_start(d_tab[:].bitcast(I32), d_words[0].rearrange("p c r -> p (c r)").bitcast(I32))
 
         n1_l = load_list("n1_l", n1)
+        nc.sync.dma_start(x_tab[:].bitcast(I32), x_words[0].rearrange("p c r -> p (c r)").bitcast(I32))
+        nc.sync.dma_start(d_tab[:].bitcast(I32), d_words[0].rearrange("p c r -> p (c r)").bitcast(I32))
         n2_l = load_list("n2_l", n2)
         n5_l = load_list("n5_l", n5)
         n3_l = load_list("n3_l", n3)
         n4_l = load_list("n4_l", n4)
-        gain = keep.tile([P, PACK], F32, name="gain")
-        nc.sync.dma_start(gain[:], gn.rearrange("(p t) o -> p (t o)", t=PACK))
         n6_l = load_list("n6_l", n6)
         n7_l = load_list("n7_l", n7)
 
-        got_bytes = keep.tile([P, 4, S], U8, name="got_bytes", align_bytes=64)
-        nc.vector.tensor_copy(got_bytes[:, 0, :], d_bytes[:].indirect(k1_l[:]))
-        nc.vector.tensor_copy(got_bytes[:, 1, :], d_bytes[:].indirect(k2_l[:]))
+        got_bytes = keep.tile([P, 4, S], U8, name="got_bytes", tag="got_bytes", align_bytes=64)
         nc.vector.tensor_copy(got_bytes[:, 2, :], x_bytes[:].indirect(offs_l[:]))
         nc.vector.tensor_copy(got_bytes[:, 3, :], x_bytes[:].indirect(hz_l[:]))
+        nc.vector.tensor_copy(got_bytes[:, 0, :], d_bytes[:].indirect(k1_l[:]))
+        nc.vector.tensor_copy(got_bytes[:, 1, :], d_bytes[:].indirect(k2_l[:]))
         got_flat = got_bytes[:].rearrange("p l s -> p (l s)").bitcast(I32)
         planes_flat = planes[:].rearrange("p l s -> p (l s)").bitcast(I32)
         for r in range(4):
             nc.scalar.dma_start(planes_flat[r:P:32, :], got_flat[8 * r : P : 32, :])
 
-        x_got = keep.tile([P, 2, S], U32, name="x_got", align_bytes=64)
-        d_got = keep.tile([P, 2, H], U32, name="d_got", align_bytes=64)
-        nc.vector.tensor_copy(x_got[:, 0, :], x_tab[:].indirect(offs_l[:]))
+        x_offs = keep.tile([P, S], U32, name="x_offs", tag="x_bytes", align_bytes=64)
+        nc.vector.tensor_copy(x_offs[:], x_tab[:].indirect(offs_l[:]))
+        x_hz = keep.tile([P, S], U32, name="x_hz", align_bytes=64)
+        x_got = (x_offs, x_hz)
+        d_got = keep.tile([P, 2, H], U32, name="d_got", tag="d_bytes", align_bytes=64)
         nc.vector.tensor_copy(d_got[:, 0, :], d_tab[:].indirect(k1_l[:]))
         nc.vector.tensor_copy(d_got[:, 1, :], d_tab[:].indirect(k2_l[:]))
 
-        d_dealt = [keep.tile([P, 2, P], U32, name=f"d_dealt{t}", align_bytes=64) for t in range(PACK)]
-        b_dealt = [keep.tile([P, 2, P], U8, name=f"b_dealt{t}", align_bytes=64) for t in range(PACK)]
-        h_ps = [psum.tile([P, S], F32, name=f"h_ps{t}") for t in range(PACK)]
+        d_dealt = [keep.tile([P, 2, P], U32, name="d_dealt0", align_bytes=64)[:]]
+        b_dealt = [keep.tile([P, 2, P], U8, name=f"b_dealt{t}", tag=f"b_dealt{t}", align_bytes=64) for t in range(PACK)]
+        h_ps = []
 
         def deal_words(t):
-            nc.vector.tensor_copy(d_dealt[t][:], d_got[:].rearrange("p l (m t) -> p l t m", t=PACK)[:, :, t, :])
+            nc.vector.tensor_copy(d_dealt[t], d_got[:].rearrange("p l (m t) -> p l t m", t=PACK)[:, :, t, :])
 
         def deal_bytes(t):
             nc.vector.tensor_copy(b_dealt[t][:], planes[:, 0:2, :].rearrange("p l (m t) -> p l t m", t=PACK)[:, :, t, :])
 
         def first_product(t):
+            h_ps.append(psum.tile([P, S], F32, name=f"h_ps{t}", tag="h_ps"))
             for l in range(2):
                 nc.tensor.matmul_mx(
                     out=h_ps[t][:],
                     lhsT=d_dealt[t][:, l, :].bitcast(FP8X4),
                     lhsT_scale=b_dealt[t][:, l, :],
-                    rhs=x_got[:, l, :].bitcast(FP8X4),
+                    rhs=x_got[l][:].bitcast(FP8X4),
                     rhs_scale=planes[:, 2 + l, :],
                     start=(l == 0),
                     stop=(l == 1),
@@ -104,27 +104,37 @@ def tile_picked_mthzncpswsendtwo_none_p_kernel(
 
         deal_words(0)
         deal_bytes(0)
-        nc.vector.tensor_copy(x_got[:, 1, :], x_tab[:].indirect(hz_l[:]))
+        nc.vector.tensor_copy(x_hz[:], x_tab[:].indirect(hz_l[:]))
         first_product(0)
+        d_rest = keep.tile([P, PACK - 1, 2, P], U32, name="d_rest", tag="got_bytes", align_bytes=64)
+        d_dealt.extend(d_rest[:, t] for t in range(PACK - 1))
 
-        w_raw = keep.tile([P, PACK, N], F32, name="w_raw", tag="big", align_bytes=64)
+        w_raw = keep.tile([P, PACK, N], F32, name="w_raw", tag="b_dealt0", align_bytes=64)
 
         h = [keep.tile([P, S], F32, name=f"h{t}") for t in range(PACK)]
-        pa = [keep.tile([P, W], F32, name=f"pa{t}", tag=f"pa{t}") for t in range(PACK)]
+        pa = [keep.tile([P, W], F32, name=f"pa{t}", tag=f"pa{t}", align_bytes=64) for t in range(PACK)]
         pb = [keep.tile([P, W], F32, name=f"pb{t}", tag=f"pb{t}") for t in range(PACK)]
-        rb = [keep.tile([P, W], F32, name=f"rb{t}") for t in range(PACK)]
         ub = [keep.tile([P, S], F32, name=f"ub{t}") for t in range(PACK)]
-        h5a = keep.tile([P, PACK, FIRST], F32, name="h5a")
+        h5a = []
 
         def larger(t):
-            nc.vector.tensor_tensor(rb[t][:], pa[t][:], pb[t][:], ALU.max)
-            nc.scalar.activation(ub[t][:].indirect(n4_l[:]), rb[t][:], COPY)
+            rb = keep.tile([P, W], F32, name=f"rb{t}", tag=f"b_dealt{t + 1}", align_bytes=64)
+            nc.vector.tensor_tensor(rb[:], pa[t][:], pb[t][:], ALU.max)
+            nc.scalar.activation(ub[t][:].indirect(n4_l[:]), rb[:], COPY)
+
+        def first_places(t, tag):
+            h5a.append(keep.tile([P, FIRST], F32, name=f"h5a{t}", tag=tag, align_bytes=64))
+            nc.scalar.activation(h5a[t][:], h[t][:].indirect(n5_l[:, 0 : FIRST // 16]), COPY)
 
         for t in range(PACK):
-            nc.vector.tensor_scalar_mul(h[t][:], h_ps[t][:], 0.0625)
+            if t == 0:
+                nc.scalar.activation(h[t][:], h_ps[t][:], COPY, scale=0.0625)
+            else:
+                nc.vector.tensor_scalar_mul(h[t][:], h_ps[t][:], 0.0625)
             nc.scalar.activation(pa[t][:], h[t][:].indirect(n1_l[:]), COPY)
             nc.vector.tensor_copy(pb[t][:], h[t][:].indirect(n2_l[:]))
-            nc.scalar.activation(h5a[:, t, :], h[t][:].indirect(n5_l[:, 0 : FIRST // 16]), COPY)
+            if t + 1 < PACK:
+                first_places(t, f"h5a{t}")
             nc.scalar.activation(ub[t][:].indirect(n3_l[:]), pb[t][:], COPY)
             if t + 1 < PACK:
                 deal_words(t + 1)
@@ -134,8 +144,11 @@ def tile_picked_mthzncpswsendtwo_none_p_kernel(
                 nc.sync.dma_start(w_raw[:], w1.rearrange("(p t) m -> p t m", t=PACK))
             if t > 0:
                 larger(t - 1)
+        first_places(PACK - 1, f"b_dealt{PACK - 1}")
         larger(PACK - 1)
 
+        gain = keep.tile([P, PACK], F32, name="gain", tag="pa1", align_bytes=64)
+        nc.sync.dma_start(gain[:], gn.rearrange("(p t) o -> p (t o)", t=PACK))
         w_bf = keep.tile([P, N, PACK], BF16, name="w_bf", align_bytes=64)
         w_codes = keep.tile([P, N], U32, name="w_codes", align_bytes=64)
         w_scale = keep.tile([P, N], U8, name="w_scale", align_bytes=64)
@@ -173,10 +186,10 @@ def tile_picked_mthzncpswsendtwo_none_p_kernel(
                 stop=True,
             )
 
-        da = keep.tile([P, PACK, FIRST], F32, name="da", tag=f"pa{PACK - 1}")
+        da = keep.tile([P, PACK, FIRST], F32, name="da", tag=f"pa{PACK - 1}", align_bytes=64)
         za = keep.tile([P, FIRST, PACK], BF16, name="za", align_bytes=64)
         for t in range(PACK):
-            nc.vector.tensor_tensor(da[:, t, :], ub[t][:, 0:FIRST], h5a[:, t, :], ALU.subtract)
+            nc.vector.tensor_tensor(da[:, t, :], ub[t][:, 0:FIRST], h5a[t][:], ALU.subtract)
             nc.vector.tensor_scalar_mul(za[:, :, t], da[:, t, :], gain[:, t : t + 1])
         nc.vector.quantize_mx(out=z_codes[:, 0:FIRST].bitcast(FP8X4), scales=z_scale[:, 0:FIRST],
                               in_=za[:].rearrange("p c t -> p (c t)"))
@@ -208,5 +221,7 @@ def tile_picked_mthzncpswsendtwo_none_p_kernel(
         for m in range(PACK):
             nc.scalar.activation(ds[m][:].indirect(n6_l[:, FIRST // 16 : S // 16]), h2b[m][:], COPY)
             nc.scalar.activation(ds2[m][:].indirect(n7_l[:, FIRST // 16 : S // 16]), h2b[m][:], COPY)
-            nc.vector.tensor_tensor(res[m][:], ds[m][:], ds2[m][:], ALU.max)
-            nc.sync.dma_start(out[m * P : (m + 1) * P, :], res[m][:])
+            pieces = [(nc.sync, 0, S)] if m + 1 < PACK else [(nc.sync, 0, S // 2), (nc.scalar, S // 2, S)]
+            for queue, c0, c1 in pieces:
+                nc.vector.tensor_tensor(res[m][:, c0:c1], ds[m][:, c0:c1], ds2[m][:, c0:c1], ALU.max)
+                queue.dma_start(out[m * P : (m + 1) * P, c0:c1], res[m][:, c0:c1])

@@ -79,46 +79,51 @@ def tile_picked_mthzncpswsendtwo_none_p_kernel(
         nc.vector.tensor_copy(d_got[:, 0, :], d_tab[:].indirect(k1_l[:]))
         nc.vector.tensor_copy(d_got[:, 1, :], d_tab[:].indirect(k2_l[:]))
 
-        d_dealt = [keep.tile([P, 2, P], U32, name="d_dealt0", align_bytes=64)[:]]
-        b_dealt = [keep.tile([P, 2, P], U8, name=f"b_dealt{t}", tag=f"b_dealt{t}", align_bytes=64) for t in range(PACK)]
-        h_ps = []
+        d_dealt, b_dealt = [], []
+        byte_tag = ("b_dealt0", "b_dealt1", "b_dealt2", "b_dealt3", "rb3")
 
         def deal_words(t):
             nc.vector.tensor_copy(d_dealt[t], d_got[:].rearrange("p l (m t) -> p l t m", t=PACK)[:, :, t, :])
 
         def deal_bytes(t):
+            b_dealt.append(keep.tile([P, 2, P], U8, name=f"b_dealt{t}", tag=byte_tag[t], align_bytes=64))
             nc.vector.tensor_copy(b_dealt[t][:], planes[:, 0:2, :].rearrange("p l (m t) -> p l t m", t=PACK)[:, :, t, :])
 
-        def first_product(t):
-            h_ps.append(psum.tile([P, S], F32, name=f"h_ps{t}", tag="h_ps"))
+        def first_product(acc, t, cols):
             for l in range(2):
                 nc.tensor.matmul_mx(
-                    out=h_ps[t][:],
+                    out=acc,
                     lhsT=d_dealt[t][:, l, :].bitcast(FP8X4),
                     lhsT_scale=b_dealt[t][:, l, :],
-                    rhs=x_got[l][:].bitcast(FP8X4),
-                    rhs_scale=planes[:, 2 + l, :],
+                    rhs=x_got[l][:, cols].bitcast(FP8X4),
+                    rhs_scale=planes[:, 2 + l, cols],
                     start=(l == 0),
                     stop=(l == 1),
                 )
 
+        d_dealt.append(keep.tile([P, 2, P], U32, name="d_dealt0", align_bytes=64)[:])
         deal_words(0)
         deal_bytes(0)
         nc.vector.tensor_copy(x_hz[:], x_tab[:].indirect(hz_l[:]))
-        first_product(0)
+        h = [keep.tile([P, S], F32, name=f"h{t}") for t in range(PACK)]
+        halves = [slice(i * S // 2, (i + 1) * S // 2) for i in range(2)]
+        h0_ps = [psum.tile([P, S // 2], F32, name=f"h0_ps{i}", tag=("h0_ps", "h_ps")[i]) for i in range(2)]
+        for i in range(2):
+            first_product(h0_ps[i][:], 0, halves[i])
+            nc.scalar.activation(h[0][:, halves[i]], h0_ps[i][:], COPY, scale=0.0625)
+
         d_rest = keep.tile([P, PACK - 1, 2, P], U32, name="d_rest", tag="got_bytes", align_bytes=64)
         d_dealt.extend(d_rest[:, t] for t in range(PACK - 1))
-
         w_raw = keep.tile([P, PACK, N], F32, name="w_raw", tag="b_dealt0", align_bytes=64)
+        nc.sync.dma_start(w_raw[:], w1.rearrange("(p t) m -> p t m", t=PACK))
 
-        h = [keep.tile([P, S], F32, name=f"h{t}") for t in range(PACK)]
         pa = [keep.tile([P, W], F32, name=f"pa{t}", tag=f"pa{t}", align_bytes=64) for t in range(PACK)]
-        pb = [keep.tile([P, W], F32, name=f"pb{t}", tag=f"pb{t}") for t in range(PACK)]
+        pb = [keep.tile([P, W], F32, name=f"pb{t}", tag=f"pb{t}", align_bytes=64) for t in range(PACK)]
         ub = [keep.tile([P, S], F32, name=f"ub{t}") for t in range(PACK)]
         h5a = []
 
         def larger(t):
-            rb = keep.tile([P, W], F32, name=f"rb{t}", tag=f"b_dealt{t + 1}", align_bytes=64)
+            rb = keep.tile([P, W], F32, name=f"rb{t}", tag=byte_tag[t + 1], align_bytes=64)
             nc.vector.tensor_tensor(rb[:], pa[t][:], pb[t][:], ALU.max)
             nc.scalar.activation(ub[t][:].indirect(n4_l[:]), rb[:], COPY)
 
@@ -126,25 +131,23 @@ def tile_picked_mthzncpswsendtwo_none_p_kernel(
             h5a.append(keep.tile([P, FIRST], F32, name=f"h5a{t}", tag=tag, align_bytes=64))
             nc.scalar.activation(h5a[t][:], h[t][:].indirect(n5_l[:, 0 : FIRST // 16]), COPY)
 
-        for t in range(PACK):
-            if t == 0:
-                nc.scalar.activation(h[t][:], h_ps[t][:], COPY, scale=0.0625)
-            else:
-                nc.vector.tensor_scalar_mul(h[t][:], h_ps[t][:], 0.0625)
+        def look_up(t):
             nc.scalar.activation(pa[t][:], h[t][:].indirect(n1_l[:]), COPY)
             nc.vector.tensor_copy(pb[t][:], h[t][:].indirect(n2_l[:]))
             if t + 1 < PACK:
                 first_places(t, f"h5a{t}")
             nc.scalar.activation(ub[t][:].indirect(n3_l[:]), pb[t][:], COPY)
-            if t + 1 < PACK:
-                deal_words(t + 1)
-                deal_bytes(t + 1)
-                first_product(t + 1)
-            if t == 0:
-                nc.sync.dma_start(w_raw[:], w1.rearrange("(p t) m -> p t m", t=PACK))
-            if t > 0:
-                larger(t - 1)
-        first_places(PACK - 1, f"b_dealt{PACK - 1}")
+
+        look_up(0)
+        for t in range(1, PACK):
+            deal_words(t)
+            deal_bytes(t)
+            h_ps = psum.tile([P, S], F32, name=f"h_ps{t}", tag="h_ps")
+            first_product(h_ps[:], t, slice(0, S))
+            nc.vector.tensor_scalar_mul(h[t][:], h_ps[:], 0.0625)
+            look_up(t)
+            larger(t - 1)
+        first_places(PACK - 1, byte_tag[PACK - 1])
         larger(PACK - 1)
 
         gain = keep.tile([P, PACK], F32, name="gain", tag="pa1", align_bytes=64)
@@ -165,7 +168,7 @@ def tile_picked_mthzncpswsendtwo_none_p_kernel(
                 in_=w_bf[:, cols, :].rearrange("p c t -> p (c t)"),
             )
 
-        h5b = keep.tile([P, PACK, REST], F32, name="h5b", tag=f"pb{PACK - 1}")
+        h5b = keep.tile([P, PACK, REST], F32, name="h5b", tag=f"pb{PACK - 1}", align_bytes=64)
         for t in range(PACK):
             nc.scalar.activation(h5b[:, t, :], h[t][:].indirect(n5_l[:, FIRST // 16 : S // 16]), COPY)
 
@@ -202,13 +205,12 @@ def tile_picked_mthzncpswsendtwo_none_p_kernel(
 
         db = keep.tile([P, PACK, REST], F32, name="db")
         zb = keep.tile([P, REST, PACK], BF16, name="zb", align_bytes=64)
+        zb_rows = keep.tile([P, PACK, REST], BF16, name="zb_rows", align_bytes=64)
         for t in range(PACK):
             nc.vector.tensor_tensor(db[:, t, :], ub[t][:, FIRST:S], h5b[:, t, :], ALU.subtract)
-        nc.vector.tensor_tensor(
-            zb[:].rearrange("p (c i) t -> p c t i", i=4),
-            db[:].rearrange("p t (c i) -> p c t i", i=4),
-            gain[:].unsqueeze(1).unsqueeze(3).broadcast_to([P, REST // 4, PACK, 4]),
-            ALU.mult,
+            nc.vector.tensor_scalar_mul(zb_rows[:, t, :], db[:, t, :], gain[:, t : t + 1])
+        nc.vector.tensor_copy(
+            zb[:].rearrange("p (c i) t -> p c t i", i=4), zb_rows[:].rearrange("p t (c i) -> p c t i", i=4)
         )
         nc.vector.quantize_mx(out=z_codes[:, FIRST:S].bitcast(FP8X4), scales=z_scale[:, FIRST:S],
                               in_=zb[:].rearrange("p c t -> p (c t)"))

from contextlib import ExitStack

import concourse.mybir as mybir

K, T, S, N, G, H, W = 512, 1024, 512, 512, 2048, 512, 256
FLOPS = 2 * K * H * S * 2 + 2 * H * N * S

F32 = mybir.dt.float32
BF16 = mybir.dt.bfloat16
I32 = mybir.dt.int32
U32 = mybir.dt.uint32
U16 = mybir.dt.uint16
U8 = mybir.dt.uint8
FP8X4 = mybir.dt.float8_e4m3fn_x4
ALU = mybir.AluOpType
COPY = mybir.ActivationFunctionType.Copy

P = 128
PACK = 4
FIRST = 128
REST = S - FIRST


def tile_picked_mthzncpswsendtwo_none_p_kernel(
    tc, x_words, x_scales, d_words, d_scales, gn, w1, offs, k1, hz, k2, n1, n2, n3, n4, n5, n6, n7, out
):
    nc = tc.nc
    with ExitStack() as ctx:
        lists = ctx.enter_context(tc.tile_pool(name="lists", bufs=1))
        keep = ctx.enter_context(tc.tile_pool(name="keep", bufs=1))
        psum = ctx.enter_context(tc.psum_pool(name="psum", bufs=1))

        def load_list(name, src):
            t = lists.tile(list(src.shape), U16, name=name)
            nc.sync.dma_start(t[:], src)
            return t

        d_bytes = keep.tile([P, G], U8, name="d_bytes", tag="d_bytes", align_bytes=64)
        x_bytes = keep.tile([P, T], U8, name="x_bytes", tag="x_bytes", align_bytes=64)
        planes = keep.tile([P, 4, S], U8, name="planes", align_bytes=64)
        nc.gpsimd.memset(x_bytes[:].bitcast(I32), 0)
        nc.vector.memset(d_bytes[:].bitcast(I32), 0)
        nc.scalar.dma_start(x_bytes[0:P:8, :].bitcast(I32), x_scales[0].bitcast(I32))
        nc.scalar.dma_start(d_bytes[0:P:8, :].bitcast(I32), d_scales[0].bitcast(I32))
        offs_l = load_list("offs_l", offs)
        hz_l = load_list("hz_l", hz)
        k1_l = load_list("k1_l", k1)
        k2_l = load_list("k2_l", k2)
        nc.vector.memset(planes[:].rearrange("p l s -> p (l s)").bitcast(I32), 0)

        x_tab = keep.tile([P, T], U32, name="x_tab", tag="x_tab", align_bytes=64)
        d_tab = keep.tile([P, G], U32, name="d_tab", tag="big", align_bytes=64)

        n1_l = load_list("n1_l", n1)
        nc.sync.dma_start(x_tab[:].bitcast(I32), x_words[0].rearrange("p c r -> p (c r)").bitcast(I32))
        nc.sync.dma_start(d_tab[:].bitcast(I32), d_words[0].rearrange("p c r -> p (c r)").bitcast(I32))
        n2_l = load_list("n2_l", n2)
        n5_l = load_list("n5_l", n5)
        n3_l = load_list("n3_l", n3)
        n4_l = load_list("n4_l", n4)
        n6_l = load_list("n6_l", n6)
        n7_l = load_list("n7_l", n7)

        got_bytes = keep.tile([P, 4, S], U8, name="got_bytes", tag="got_bytes", align_bytes=64)
        nc.vector.tensor_copy(got_bytes[:, 2, :], x_bytes[:].indirect(offs_l[:]))
        nc.vector.tensor_copy(got_bytes[:, 3, :], x_bytes[:].indirect(hz_l[:]))
        nc.vector.tensor_copy(got_bytes[:, 0, :], d_bytes[:].indirect(k1_l[:]))
        nc.vector.tensor_copy(got_bytes[:, 1, :], d_bytes[:].indirect(k2_l[:]))
        got_flat = got_bytes[:].rearrange("p l s -> p (l s)").bitcast(I32)
        planes_flat = planes[:].rearrange("p l s -> p (l s)").bitcast(I32)
        for r in range(4):
            nc.scalar.dma_start(planes_flat[r:P:32, :], got_flat[8 * r : P : 32, :])

        x_offs = keep.tile([P, S], U32, name="x_offs", tag="x_bytes", align_bytes=64)
        nc.vector.tensor_copy(x_offs[:], x_tab[:].indirect(offs_l[:]))
        x_hz = keep.tile([P, S], U32, name="x_hz", align_bytes=64)
        x_got = (x_offs, x_hz)
        d_got = keep.tile([P, 2, H], U32, name="d_got", tag="d_bytes", align_bytes=64)
        nc.vector.tensor_copy(d_got[:, 0, :], d_tab[:].indirect(k1_l[:]))
        nc.vector.tensor_copy(d_got[:, 1, :], d_tab[:].indirect(k2_l[:]))

        d_dealt, b_dealt = [], []
        byte_tag = ("b_dealt0", "b_dealt1", "b_dealt2", "b_dealt3", "rb3")

        def deal_words(t):
            nc.vector.tensor_copy(d_dealt[t], d_got[:].rearrange("p l (m t) -> p l t m", t=PACK)[:, :, t, :])

        def deal_bytes(t):
            b_dealt.append(keep.tile([P, 2, P], U8, name=f"b_dealt{t}", tag=byte_tag[t], align_bytes=64))
            nc.vector.tensor_copy(b_dealt[t][:], planes[:, 0:2, :].rearrange("p l (m t) -> p l t m", t=PACK)[:, :, t, :])

        def first_product(acc, t, cols):
            for l in range(2):
                nc.tensor.matmul_mx(
                    out=acc,
                    lhsT=d_dealt[t][:, l, :].bitcast(FP8X4),
                    lhsT_scale=b_dealt[t][:, l, :],
                    rhs=x_got[l][:, cols].bitcast(FP8X4),
                    rhs_scale=planes[:, 2 + l, cols],
                    start=(l == 0),
                    stop=(l == 1),
                )

        d_dealt.append(keep.tile([P, 2, P], U32, name="d_dealt0", align_bytes=64)[:])
        deal_words(0)
        deal_bytes(0)
        nc.vector.tensor_copy(x_hz[:], x_tab[:].indirect(hz_l[:]))
        h = [keep.tile([P, S], F32, name=f"h{t}") for t in range(PACK)]
        halves = [slice(i * S // 2, (i + 1) * S // 2) for i in range(2)]
        h0_ps = [psum.tile([P, S // 2], F32, name=f"h0_ps{i}", tag=("h0_ps", "h_ps")[i]) for i in range(2)]
        for i in range(2):
            first_product(h0_ps[i][:], 0, halves[i])
            nc.scalar.activation(h[0][:, halves[i]], h0_ps[i][:], COPY, scale=0.0625)

        d_rest = keep.tile([P, PACK - 1, 2, P], U32, name="d_rest", tag="got_bytes", align_bytes=64)
        d_dealt.extend(d_rest[:, t] for t in range(PACK - 1))
        w_raw = keep.tile([P, PACK, N], F32, name="w_raw", tag="b_dealt0", align_bytes=64)
        nc.sync.dma_start(w_raw[:], w1.rearrange("(p t) m -> p t m", t=PACK))

        pa = [keep.tile([P, W], F32, name=f"pa{t}", tag=f"pa{t}", align_bytes=64) for t in range(PACK)]
        pb = [keep.tile([P, W], F32, name=f"pb{t}", tag=f"pb{t}", align_bytes=64) for t in range(PACK)]
        ub = [keep.tile([P, S], F32, name=f"ub{t}") for t in range(PACK)]
        h5a = []

        def larger(t):
            rb = keep.tile([P, W], F32, name=f"rb{t}", tag=byte_tag[t + 1], align_bytes=64)
            nc.vector.tensor_tensor(rb[:], pa[t][:], pb[t][:], ALU.max)
            nc.scalar.activation(ub[t][:].indirect(n4_l[:]), rb[:], COPY)

        def first_places(t, tag):
            h5a.append(keep.tile([P, FIRST], F32, name=f"h5a{t}", tag=tag, align_bytes=64))
            nc.scalar.activation(h5a[t][:], h[t][:].indirect(n5_l[:, 0 : FIRST // 16]), COPY)

        def look_up(t):
            nc.scalar.activation(pa[t][:], h[t][:].indirect(n1_l[:]), COPY)
            nc.vector.tensor_copy(pb[t][:], h[t][:].indirect(n2_l[:]))
            if t + 1 < PACK:
                first_places(t, f"h5a{t}")
            nc.scalar.activation(ub[t][:].indirect(n3_l[:]), pb[t][:], COPY)

        look_up(0)
        for t in range(1, PACK):
            deal_words(t)
            deal_bytes(t)
            h_ps = psum.tile([P, S], F32, name=f"h_ps{t}", tag="h_ps")
            first_product(h_ps[:], t, slice(0, S))
            nc.vector.tensor_scalar_mul(h[t][:], h_ps[:], 0.0625)
            look_up(t)
            larger(t - 1)
        first_places(PACK - 1, byte_tag[PACK - 1])
        larger(PACK - 1)

        gain = keep.tile([P, PACK], F32, name="gain", tag="pa1", align_bytes=64)
        nc.sync.dma_start(gain[:], gn.rearrange("(p t) o -> p (t o)", t=PACK))
        w_bf = keep.tile([P, N, PACK], BF16, name="w_bf", align_bytes=64)
        w_codes = keep.tile([P, N], U32, name="w_codes", align_bytes=64)
        w_scale = keep.tile([P, N], U8, name="w_scale", align_bytes=64)
        for half in range(2):
            cols = slice(half * 256, (half + 1) * 256)
            nc.vector.tensor_copy(
                w_bf[:, cols, :].rearrange("p (c i) t -> p c t i", i=4),
                w_raw[:, :, cols].rearrange("p t (c i) -> p c t i", i=4),
            )
        for half in range(2):
            cols = slice(half * 256, (half + 1) * 256)
            nc.vector.quantize_mx(
                out=w_codes[:, cols].bitcast(FP8X4), scales=w_scale[:, cols],
                in_=w_bf[:, cols, :].rearrange("p c t -> p (c t)"),
            )

        h5b = keep.tile([P, PACK, REST], F32, name="h5b", tag=f"pb{PACK - 1}", align_bytes=64)
        for t in range(PACK):
            nc.scalar.activation(h5b[:, t, :], h[t][:].indirect(n5_l[:, FIRST // 16 : S // 16]), COPY)

        z_codes = keep.tile([P, S], U32, name="z_codes", align_bytes=64)
        z_scale = keep.tile([P, S], U8, name="z_scale", align_bytes=64)
        h2_ps = [psum.tile([P, S], F32, name=f"h2_ps{m}") for m in range(PACK)]
        ds = [keep.tile([P, S], F32, name=f"ds{m}") for m in range(PACK)]
        ds2 = [keep.tile([P, S], F32, name=f"dt{m}") for m in range(PACK)]

        def second_product(m, c0, c1):
            nc.tensor.matmul_mx(
                out=h2_ps[m][:, c0:c1],
                lhsT=w_codes[:, m * P : (m + 1) * P].bitcast(FP8X4),
                lhsT_scale=w_scale[:, m * P : (m + 1) * P],
                rhs=z_codes[:, c0:c1].bitcast(FP8X4),
                rhs_scale=z_scale[:, c0:c1],
                start=True,
                stop=True,
            )

        da = keep.tile([P, PACK, FIRST], F32, name="da", tag=f"pa{PACK - 1}", align_bytes=64)
        za = keep.tile([P, FIRST, PACK], BF16, name="za", align_bytes=64)
        for t in range(PACK):
            nc.vector.tensor_tensor(da[:, t, :], ub[t][:, 0:FIRST], h5a[t][:], ALU.subtract)
            nc.vector.tensor_scalar_mul(za[:, :, t], da[:, t, :], gain[:, t : t + 1])
        nc.vector.quantize_mx(out=z_codes[:, 0:FIRST].bitcast(FP8X4), scales=z_scale[:, 0:FIRST],
                              in_=za[:].rearrange("p c t -> p (c t)"))
        h2a = [keep.tile([P, FIRST], F32, name=f"h2a{m}") for m in range(PACK)]
        for m in range(PACK):
            second_product(m, 0, FIRST)
            nc.vector.tensor_copy(h2a[m][:], h2_ps[m][:, 0:FIRST])
            nc.scalar.activation(ds[m][:].indirect(n6_l[:, 0 : FIRST // 16]), h2a[m][:], COPY)
            nc.scalar.activation(ds2[m][:].indirect(n7_l[:, 0 : FIRST // 16]), h2a[m][:], COPY)

        db = keep.tile([P, PACK, REST], F32, name="db")
        zb = keep.tile([P, REST, PACK], BF16, name="zb", align_bytes=64)
        zb_rows = keep.tile([P, PACK, REST], BF16, name="zb_rows", align_bytes=64)
        for t in range(PACK):
            nc.vector.tensor_tensor(db[:, t, :], ub[t][:, FIRST:S], h5b[:, t, :], ALU.subtract)
            nc.vector.tensor_scalar_mul(zb_rows[:, t, :], db[:, t, :], gain[:, t : t + 1])
        nc.vector.tensor_copy(
            zb[:].rearrange("p (c i) t -> p c t i", i=4), zb_rows[:].rearrange("p t (c i) -> p c t i", i=4)
        )
        nc.vector.quantize_mx(out=z_codes[:, FIRST:S].bitcast(FP8X4), scales=z_scale[:, FIRST:S],
                              in_=zb[:].rearrange("p c t -> p (c t)"))
        h2b = [keep.tile([P, REST], F32, name=f"h2b{m}") for m in range(PACK)]
        res = [keep.tile([P, S], F32, name=f"res{m}") for m in range(PACK)]
        for m in range(PACK):
            second_product(m, FIRST, FIRST + 256)
            second_product(m, FIRST + 256, S)
            nc.vector.tensor_copy(h2b[m][:], h2_ps[m][:, FIRST:S])
        for m in range(PACK):
            nc.scalar.activation(ds[m][:].indirect(n6_l[:, FIRST // 16 : S // 16]), h2b[m][:], COPY)
            nc.scalar.activation(ds2[m][:].indirect(n7_l[:, FIRST // 16 : S // 16]), h2b[m][:], COPY)
            pieces = [(nc.sync, 0, S)] if m + 1 < PACK else [(nc.sync, 0, S // 2), (nc.scalar, S // 2, S)]
            for queue, c0, c1 in pieces:
                nc.vector.tensor_tensor(res[m][:, c0:c1], ds[m][:, c0:c1], ds2[m][:, c0:c1], ALU.max)
                queue.dma_start(out[m * P : (m + 1) * P, c0:c1], res[m][:, c0:c1])
